import numpy as np, ml_dtypes
CORES = [5,13,29,37,53,69,77,101,133,141,157,165,181,197,205,229]
N = 16
import mx_ref
NC, ROOT = 128, 6
C = np.float32(0.047)
BF = ml_dtypes.bfloat16
def cut(t, i, w=512):
    return t[:, w * i:w * i + w]
def tile(rs):
    return np.stack(rs, axis=2).reshape(128, -1).astype(BF)
def pick(b):
    s = np.zeros((128, 128, 4), np.float32)
    s[np.arange(128), np.arange(128), b] = 1.0
    return mx_ref.quantize(s.reshape(128, 512).astype(BF))
def pk(c, s, i=0):
    return (np.ascontiguousarray(c[:, 512 * i:512 * i + 512]), mx_ref.live(s[:, 128 * i:128 * i + 128]))
def inputs(rng, e, E):
    def f(*shape):
        v = (rng.standard_normal(shape, dtype=np.float32) * np.exp2(rng.integers(-2, 3, shape[:-1] + (1,)))).astype(BF)
        return mx_ref.spread((v.astype(np.float32) * np.exp2(rng.integers(-E, E + 1, shape[:-2] + (1, 1))).astype(np.float32)).astype(BF), rng, e)
    def packed(k):
        c = np.zeros((N, 128, k * 512), np.uint8); s = np.zeros((N, 128, k * 128), np.uint8)
        for r in range(N):
            for i in range(k):
                a, b = mx_ref.quantize(f(128, 512)); c[r][:, 512 * i:512 * i + 512] = a; s[r][:, 128 * i:128 * i + 128] = mx_ref.plane(b, rng)
        return c, s
    d = {}
    d["wc"], d["ws"] = packed(1)
    d["a"] = f(N, 128, 512)
    d["bb"] = f(N, 128, 4 * 512)
    d["x"] = f(N, 128, 4 * NC)
    return d
def setup_inputs(rng):
    return inputs(rng, 0, 0)
def setup_inputs_blocks(rng):
    return inputs(rng, 2, 0)
def setup_inputs_wide(rng):
    return inputs(rng, 0, 3)
def reference(wc, ws, a, bb, x):
    S = [pick(t) for t in range(4)]; A = mx_ref.quantize(a[ROOT])
    V = [mx_ref.quantize(tile([mx_ref.matmul(S[t], pk(wc[j], ws[j])) + mx_ref.matmul(mx_ref.quantize(cut(bb[j], t)), A) * C for t in range(4)])) for j in range(N)]
    y = np.zeros((N, 128, N * NC), np.float32)
    for r in range(N):
        X = mx_ref.quantize(x[r])
        for j in range(N):
            y[r][:, NC * j:NC * j + NC] = mx_ref.matmul(V[j], X)
    return {"y": y}

@@ -1,0 +1,235 @@
+from concourse.bass import DstId, RemoteDMATransfer
+from concourse.mybir import dt, AluOpType, ActivationFunctionType
+
+N = 16
+K = 128
+FP8 = "float8_e4m3fn_x4"
+WORLD = 256
+FAR = 7
+DUE_A = ((-1.9, -0.9, 0.4), (-1.8, -0.2, 1.3, 2.2), (-1.9, 0.2, 1.0), (-0.2, 0.8, 2.3), (1.0, 1.2))
+DUE_V = ((-1.9, -1.1, -0.2), (-1.1, -0.2, 0.5, 1.3), (-0.8, 0.0, 0.7), (-0.1, 0.5, 1.2), (0.6, 0.7))
+DUE_ROOT = -3.3
+
+SCRATCH = {
+    "a16": ("sbuf", [128, 4 * K], "bfloat16"),
+    "b16": ("sbuf", [128, 16 * K], "bfloat16"),
+    "x16": ("sbuf", [128, 4 * K], "bfloat16"),
+    "sel": ("sbuf", [128, 8 * K], "bfloat16"),
+    "v16": ("sbuf", [128, 4 * K], "bfloat16"),
+    "acode": ("sbuf", [128, K], FP8), "aplane": ("sbuf", [128, K], "uint8"),
+    "bcode": ("sbuf", [128, 4 * K], FP8), "bplane": ("sbuf", [128, 4 * K], "uint8"),
+    "xcode": ("sbuf", [128, K], FP8), "xplane": ("sbuf", [128, K], "uint8"),
+    "wcode": ("sbuf", [128, K], FP8), "wplane": ("sbuf", [128, K], "uint8"),
+    "scode": ("sbuf", [128, 4 * K], FP8), "splane": ("sbuf", [128, 4 * K], "uint8"),
+    "vcode": ("sbuf", [128, N * K], FP8), "vplane": ("sbuf", [128, N * K], "uint8"),
+    "scaled": ("sbuf", [128, 4 * K], "float32"),
+    "yo": ("sbuf", [128, N * K], "float32"),
+    "ps": ("psum", [128, 512 * 8], "float32"),
+}
+SEMAPHORES = (["ld_a", "ld_w", "ld_b", "ld_x", "ones", "diag", "qs", "qa", "qb", "qx", "qv",
+               "s_in", "a_in", "hop_ac", "hop_ap", "hop_vc", "hop_vp", "sent", "dmm", "added", "st"]
+              + ["arr%d" % j for j in range(N)] + ["mm%d" % b for b in range(4)] + ["mu%d" % b for b in range(4)]
+              + ["ym%d" % t for t in range(N)] + ["yc%d" % t for t in range(N)])
+
+
+def chip_of(topo, c):
+    return (topo.host(c), topo.chip(c))
+
+
+def helpers(T, topo, rc):
+    here = [c for c in range(WORLD) if c != rc and chip_of(topo, c) == chip_of(topo, rc)
+            and all(topo.may_write(c, d) for d in T.cores if d != rc)]
+    return [c for c in here if topo.die(c) != topo.die(rc)], [c for c in here if topo.die(c) == topo.die(rc)]
+
+
+def plan(T, topo, s):
+    rc = T.cores[s]
+    far, near = helpers(T, topo, rc)
+    fd = [(s + k) % N for k in range(1, FAR + 1)]
+    nd = [(s + k) % N for k in range(FAR + 1, N)]
+    own = [d for d in nd if topo.may_write(rc, T.cores[d])][:3]
+    rest = [d for d in nd if d not in own]
+    return [(rc, own), (far[0], fd[:4]), (near[0], rest[:3]), (far[1], fd[4:]), (near[1], rest[3:])]
+
+
+def due(T, topo, s, d):
+    def at(src, dst, table):
+        for (_, dests), row in zip(plan(T, topo, src), table):
+            if dst in dests:
+                return row[dests.index(dst)]
+        return DUE_ROOT
+    return at(T.root, s, DUE_A) + at(s, d, DUE_V)
+
+
+def own_picks(T, r):
+    p = (r + N // 2) % N
+    if r == T.root:
+        return [], p, [], [0, 1]
+    if p == T.root:
+        return [0, 1], p, [0, 1], []
+    return ([0], p, [0], [1]) if r < p else ([1], p, [1], [0])
+
+
+def u8(buf, a, b):
+    return buf[:, a:b].bitcast(dt.uint8)
+
+
+def rank_program(g, core, T, topo):
+    mine = [s for s in range(N) if chip_of(topo, T.cores[s]) == chip_of(topo, core)]
+    if not mine:
+        return
+    s = mine[0]
+    vroute, aroute = plan(T, topo, s), plan(T, topo, T.root)
+    if core not in [c for c, _ in vroute]:
+        return
+    rc, root, sem = T.cores[s], s == T.root, T.sem
+    hs = [c for c, _ in vroute[1:]]
+    vdst = [T.cores[d] for d in dict(vroute)[core]]
+    adst = [T.cores[d] for d in dict(aroute).get(core, [])]
+    on, off = topo.mask(rc, hs[0]), topo.mask(core, vdst[0])
+    n_on, n_off = bin(on).count("1"), bin(off).count("1")
+    sent = [0]
+
+    def send(view, dests, rsem, m):
+        ids = []
+        for d in dests:
+            rid, pid = topo.addr(d, core)
+            ids.append(DstId(rid=rid, pnc=pid))
+        g.remote_dma_fused([RemoteDMATransfer(dst_ids=ids, dma_engine_mask=m, remote_sem=rsem, srcs=[view],
+                                              dsts=[view] * len(dests))], local_sem=sem.sent)
+        sent[0] += bin(m).count("1")
+
+    def make_picks(tiles):
+        if not tiles:
+            return
+        g.vector.memset(T.sel[:, 0:4 * K * len(tiles)], 1.0).then_inc(sem.ones, 1)
+        g.wait_ge(sem.ones, 1)
+        for i, b in enumerate(tiles):
+            v = T.sel[:, 4 * K * i:4 * K * (i + 1)]
+            g.affine_select(v, v, [[1, 4 * K]], AluOpType.is_equal, 0.0, -b, -4).then_inc(sem.diag, 1)
+        g.vector.wait_ge(sem.diag, len(tiles))
+        for i, b in enumerate(tiles):
+            g.vector.quantize_mx(T.scode[:, K * b:K * b + K], T.splane[:, K * b:K * b + K],
+                                 T.sel[:, 4 * K * i:4 * K * (i + 1)]).then_inc(sem.qs, 1)
+        g.wait_ge(sem.qs, len(tiles))
+
+    vt = (T.vplane[:, K * s:K * s + K], u8(T.vcode, K * s, K * s + K))
+    at = (T.aplane[:, 0:K], u8(T.acode, 0, K))
+    vhop, ahop = (sem.hop_vp, sem.hop_vc), (sem.hop_ap, sem.hop_ac)
+
+    if core != rc:
+        i = hs.index(core)
+        b, lo = 2 + i // 2, (i % 2) * (K // 2)
+        make_picks([b])
+        lo += K * b
+        send(u8(T.scode, lo, lo + K // 2), [rc], sem.s_in, off)
+        send(T.splane[:, lo:lo + K // 2], [rc], sem.s_in, off)
+        if root:
+            for w in (0, 1):
+                g.wait_ge(ahop[w], n_on)
+                send(at[w], adst, sem.a_in, off)
+        for w in (0, 1):
+            g.wait_ge(vhop[w], n_on)
+            send(vt[w], vdst, sem["arr%d" % s], off)
+        g.wait_ge(sem.sent, sent[0])
+        return
+
+    def spread(t, dests, hop, rsem):
+        for w in (0, 1):
+            send(t[w], hs, hop[w], on)
+        for w in (0, 1):
+            send(t[w], dests, rsem, off)
+
+    if root:
+        g.sync.dma_start(T.a16[:], T.a[:]).then_inc(sem.ld_a, 16)
+        g.sync.wait_ge(sem.ld_a, 16)
+    g.sync.dma_start(u8(T.wcode, 0, K), T.wc[:]).then_inc(sem.ld_w, 16)
+    g.sync.dma_start(T.wplane[:], T.ws[:]).then_inc(sem.ld_w, 16)
+    g.sync.dma_start(T.b16[:], T.bb[:]).then_inc(sem.ld_b, 16)
+    g.sync.dma_start(T.x16[:], T.x[:]).then_inc(sem.ld_x, 16)
+
+    if root:
+        g.vector.wait_ge(sem.ld_a, 16)
+        g.vector.quantize_mx(T.acode[:], T.aplane[:], T.a16[:]).then_inc(sem.qa, 1)
+        g.wait_ge(sem.qa, 1)
+        spread(at, adst, ahop, sem.a_in)
+    tiles, peer, give, get = own_picks(T, s)
+    make_picks(tiles)
+    for b in give:
+        send(u8(T.scode, K * b, K * b + K), [T.cores[peer]], sem.s_in, off)
+        send(T.splane[:, K * b:K * b + K], [T.cores[peer]], sem.s_in, off)
+
+    g.vector.wait_ge(sem.ld_b, 16)
+    for b in range(4):
+        g.vector.quantize_mx(T.bcode[:, K * b:K * b + K], T.bplane[:, K * b:K * b + K],
+                             T.b16[:, 4 * K * b:4 * K * (b + 1)]).then_inc(sem.qb, 1)
+    g.vector.wait_ge(sem.ld_x, 16)
+    g.vector.quantize_mx(T.xcode[:], T.xplane[:], T.x16[:]).then_inc(sem.qx, 1)
+
+    def bank(i):
+        return T.ps[:, 512 * i:512 * i + K]
+
+    te = g.tensor
+    te.wait_ge(sem.ld_w, 32)
+    if tiles:
+        te.wait_ge(sem.qs, len(tiles))
+    te.wait_ge(sem.s_in, 2 * n_off * (len(get) + len(hs)))
+    for b in range(4):
+        te.matmul_mx(bank(b), T.scode[:, K * b:K * b + K], T.splane[:, K * b:K * b + K], T.wcode[:], T.wplane[:],
+                     True, True).then_inc(sem.dmm, 1)
+    te.wait_ge(sem.qb, 4)
+    if root:
+        te.wait_ge(sem.qa, 1)
+    else:
+        te.wait_ge(sem.a_in, 2 * n_off)
+    for b in range(4):
+        te.matmul_mx(bank(4 + b), T.bcode[:, K * b:K * b + K], T.bplane[:, K * b:K * b + K], T.acode[:], T.aplane[:],
+                     True, True).then_inc(sem["mm%d" % b], 1)
+
+    for b in range(4):
+        g.scalar.wait_ge(sem["mm%d" % b], 1)
+        g.scalar.activation(T.scaled[:, K * b:K * b + K], bank(4 + b), ActivationFunctionType.Copy,
+                            scale=0.047).then_inc(sem["mu%d" % b], 1)
+    g.vector.wait_ge(sem.dmm, 4)
+    for b in range(4):
+        g.vector.wait_ge(sem["mu%d" % b], 1)
+        g.vector.tensor_tensor(T.v16[:, b:4 * K:4], bank(b), T.scaled[:, K * b:K * b + K],
+                               AluOpType.add).then_inc(sem.added, 1)
+    g.vector.wait_ge(sem.added, 4)
+    g.vector.quantize_mx(T.vcode[:, K * s:K * s + K], T.vplane[:, K * s:K * s + K], T.v16[:]).then_inc(sem.qv, 1)
+    g.wait_ge(sem.qv, 1)
+    spread(vt, vdst, vhop, sem["arr%d" % s])
+
+    order = [s] + [j for _, j in sorted((due(T, topo, j, s), j) for j in range(N) if j != s)]
+    te.wait_ge(sem.qx, 1)
+    for t, j in enumerate(order):
+        if j == s:
+            te.wait_ge(sem.qv, 1)
+        else:
+            te.wait_ge(sem["arr%d" % j], 2 * n_off)
+        if t >= 8:
+            te.wait_ge(sem["yc%d" % (t - 8)], 1)
+        te.matmul_mx(bank(t % 8), T.vcode[:, K * j:K * j + K], T.vplane[:, K * j:K * j + K], T.xcode[:], T.xplane[:],
+                     True, True).then_inc(sem["ym%d" % t], 1)
+        dst = T.yo[:, K * j:K * j + K]
+        if t % 2:
+            g.scalar.wait_ge(sem["ym%d" % t], 1)
+            g.scalar.activation(dst, bank(t % 8), ActivationFunctionType.Copy).then_inc(sem["yc%d" % t], 1)
+        else:
+            g.vector.wait_ge(sem["ym%d" % t], 1)
+            g.vector.tensor_copy(dst, bank(t % 8)).then_inc(sem["yc%d" % t], 1)
+
+    left, stores = list(order), 0
+    while left:
+        grp = [left.pop(0)]
+        near = [q for q in left[:3] if abs(q - grp[0]) == 1]
+        if near and len(left) > 1:
+            grp.append(near[0])
+            left.remove(near[0])
+        for q in grp:
+            g.sync.wait_ge(sem["yc%d" % order.index(q)], 1)
+        lo, hi = K * min(grp), K * (max(grp) + 1)
+        g.sync.dma_start(T.y[:, lo:hi], T.yo[:, lo:hi]).then_inc(sem.st, 16)
+        stores += 1
+    g.sync.wait_ge(sem.st, 16 * stores)
+    g.wait_ge(sem.sent, sent[0])

@@ -5,16 +5,13 @@ N = 16
 K = 128
 FP8 = "float8_e4m3fn_x4"
 WORLD = 256
-FAR = 7
-DUE_A = ((-1.9, -0.9, 0.4), (-1.8, -0.2, 1.3, 2.2), (-1.9, 0.2, 1.0), (-0.2, 0.8, 2.3), (1.0, 1.2))
-DUE_V = ((-1.9, -1.1, -0.2), (-1.1, -0.2, 0.5, 1.3), (-0.8, 0.0, 0.7), (-0.1, 0.5, 1.2), (0.6, 0.7))
-DUE_ROOT = -3.3
+ON, OFF, HOP = (0.12, 0.22), (0.25, 0.5), 0.9
 
 SCRATCH = {
     "a16": ("sbuf", [128, 4 * K], "bfloat16"),
     "b16": ("sbuf", [128, 16 * K], "bfloat16"),
     "x16": ("sbuf", [128, 4 * K], "bfloat16"),
-    "sel": ("sbuf", [128, 8 * K], "bfloat16"),
+    "sel": ("sbuf", [128, 4 * K], "bfloat16"),
     "v16": ("sbuf", [128, 4 * K], "bfloat16"),
     "acode": ("sbuf", [128, K], FP8), "aplane": ("sbuf", [128, K], "uint8"),
     "bcode": ("sbuf", [128, 4 * K], FP8), "bplane": ("sbuf", [128, 4 * K], "uint8"),
@@ -27,7 +24,7 @@ SCRATCH = {
     "ps": ("psum", [128, 512 * 8], "float32"),
 }
 SEMAPHORES = (["ld_a", "ld_w", "ld_b", "ld_x", "ones", "diag", "qs", "qa", "qb", "qx", "qv",
-               "s_in", "a_in", "hop_ac", "hop_ap", "hop_vc", "hop_vp", "sent", "dmm", "added", "st"]
+               "s_in", "hop_s", "a_in", "hop_ac", "hop_ap", "hop_vc", "hop_vp", "sent", "dmm", "added", "st"]
               + ["arr%d" % j for j in range(N)] + ["mm%d" % b for b in range(4)] + ["mu%d" % b for b in range(4)]
               + ["ym%d" % t for t in range(N)] + ["yc%d" % t for t in range(N)])
 
@@ -36,38 +33,50 @@ def chip_of(topo, c):
     return (topo.host(c), topo.chip(c))
 
 
-def helpers(T, topo, rc):
-    here = [c for c in range(WORLD) if c != rc and chip_of(topo, c) == chip_of(topo, rc)
-            and all(topo.may_write(c, d) for d in T.cores if d != rc)]
-    return [c for c in here if topo.die(c) != topo.die(rc)], [c for c in here if topo.die(c) == topo.die(rc)]
-
-
 def plan(T, topo, s):
     rc = T.cores[s]
-    far, near = helpers(T, topo, rc)
-    fd = [(s + k) % N for k in range(1, FAR + 1)]
-    nd = [(s + k) % N for k in range(FAR + 1, N)]
-    own = [d for d in nd if topo.may_write(rc, T.cores[d])][:3]
-    rest = [d for d in nd if d not in own]
-    return [(rc, own), (far[0], fd[:4]), (near[0], rest[:3]), (far[1], fd[4:]), (near[1], rest[3:])]
+    others = [(s + k) % N for k in range(1, N)]
+    here = [c for c in range(WORLD) if c != rc and chip_of(topo, c) == chip_of(topo, rc)]
+    free = [c for c in here if all(topo.may_write(c, T.cores[d]) for d in others)]
+    def by_die(cores):
+        return [[c for c in cores if (topo.die(c) == topo.die(rc)) == near] for near in (False, True)]
+    (f0, f1), (n0, n1) = by_die(free)
+    bf, bn = by_die([c for c in here if c not in free])
+    same = [d for d in others if topo.may_write(rc, T.cores[d])]
+    cross = [d for d in others if d not in same]
+    if len(cross) < len(same):
+        fs, ns, fc, nc = same[:4], same[4:], cross[:3], cross[3:]
+    else:
+        fs, ns, fc, nc = same[:2], same[2:], cross[:5], cross[5:]
+    codes = {f0: fc[:3], n0: nc[:3], bf[0]: fs[:2], bn[0]: ns[:3], bf[1]: fs[2:], f1: fc[3:], n1: nc[3:], rc: ns[3:]}
+    if codes[f1]:
+        planes = {f1: nc, n1: fc, rc: same}
+    else:
+        planes = {f1: nc + ns, n1: fc + fs}
+    route = [(c, planes.get(c, []), codes[c]) for c in [rc, f0, n0, bf[0], bn[0], bf[1], f1, n1]]
+    return [r for r in route if r[1] or r[2]]
 
 
-def due(T, topo, s, d):
-    def at(src, dst, table):
-        for (_, dests), row in zip(plan(T, topo, src), table):
-            if dst in dests:
-                return row[dests.index(dst)]
-        return DUE_ROOT
-    return at(T.root, s, DUE_A) + at(s, d, DUE_V)
+def eta(route):
+    t, due, start = 0.0, {}, {}
+    for w in (0, 1):
+        for c, *lists in route[1:]:
+            if lists[w]:
+                t += ON[w]
+                start[c, w] = t + HOP
+    for c, *lists in route:
+        u = t
+        for w in (0, 1):
+            u = max(u, start.get((c, w), 0.0))
+            for d in lists[w]:
+                u += OFF[w]
+                due[d] = max(due.get(d, 0.0), u)
+    return due
 
 
-def own_picks(T, r):
+def own_pick(r):
     p = (r + N // 2) % N
-    if r == T.root:
-        return [], p, [], [0, 1]
-    if p == T.root:
-        return [0, 1], p, [0, 1], []
-    return ([0], p, [0], [1]) if r < p else ([1], p, [1], [0])
+    return (0 if r < p else 1), p
 
 
 def u8(buf, a, b):
@@ -80,17 +89,20 @@ def rank_program(g, core, T, topo):
         return
     s = mine[0]
     vroute, aroute = plan(T, topo, s), plan(T, topo, T.root)
-    if core not in [c for c, _ in vroute]:
+    vdst = [[T.cores[d] for d in ds] for c, *lists in vroute if c == core for ds in lists]
+    adst = [[T.cores[d] for d in ds] for c, *lists in aroute if c == core for ds in lists]
+    if not vdst:
         return
     rc, root, sem = T.cores[s], s == T.root, T.sem
-    hs = [c for c, _ in vroute[1:]]
-    vdst = [T.cores[d] for d in dict(vroute)[core]]
-    adst = [T.cores[d] for d in dict(aroute).get(core, [])]
-    on, off = topo.mask(rc, hs[0]), topo.mask(core, vdst[0])
+    hs = [c for c, _, _ in vroute[1:]]
+    hop_to = [[c for c, *lists in vroute[1:] if lists[w]] for w in (0, 1)]
+    on, off = topo.mask(rc, hs[0]), topo.mask(core, (vdst[0] + vdst[1])[0])
     n_on, n_off = bin(on).count("1"), bin(off).count("1")
     sent = [0]
 
     def send(view, dests, rsem, m):
+        if not dests:
+            return
         ids = []
         for d in dests:
             rid, pid = topo.addr(d, core)
@@ -99,65 +111,65 @@ def rank_program(g, core, T, topo):
                                               dsts=[view] * len(dests))], local_sem=sem.sent)
         sent[0] += bin(m).count("1")
 
-    def make_picks(tiles):
-        if not tiles:
-            return
-        g.vector.memset(T.sel[:, 0:4 * K * len(tiles)], 1.0).then_inc(sem.ones, 1)
+    def make_pick(b):
+        g.vector.memset(T.sel[:], 0.0).then_inc(sem.ones, 1)
         g.wait_ge(sem.ones, 1)
-        for i, b in enumerate(tiles):
-            v = T.sel[:, 4 * K * i:4 * K * (i + 1)]
-            g.affine_select(v, v, [[1, 4 * K]], AluOpType.is_equal, 0.0, -b, -4).then_inc(sem.diag, 1)
-        g.vector.wait_ge(sem.diag, len(tiles))
-        for i, b in enumerate(tiles):
-            g.vector.quantize_mx(T.scode[:, K * b:K * b + K], T.splane[:, K * b:K * b + K],
-                                 T.sel[:, 4 * K * i:4 * K * (i + 1)]).then_inc(sem.qs, 1)
-        g.wait_ge(sem.qs, len(tiles))
+        v = T.sel[:, b:4 * K:4]
+        g.affine_select(v, v, [[1, K]], AluOpType.not_equal, 1.0, 0, -1).then_inc(sem.diag, 1)
+        g.vector.wait_ge(sem.diag, 1)
+        g.vector.quantize_mx(T.scode[:, K * b:K * b + K], T.splane[:, K * b:K * b + K], T.sel[:]).then_inc(sem.qs, 1)
+        g.wait_ge(sem.qs, 1)
 
     vt = (T.vplane[:, K * s:K * s + K], u8(T.vcode, K * s, K * s + K))
     at = (T.aplane[:, 0:K], u8(T.acode, 0, K))
     vhop, ahop = (sem.hop_vp, sem.hop_vc), (sem.hop_ap, sem.hop_ac)
+    pick, peer = own_pick(s)
+    pick_codes = u8(T.scode, K * pick, K * pick + K)
 
     if core != rc:
-        i = hs.index(core)
-        b, lo = 2 + i // 2, (i % 2) * (K // 2)
-        make_picks([b])
-        lo += K * b
-        send(u8(T.scode, lo, lo + K // 2), [rc], sem.s_in, off)
-        send(T.splane[:, lo:lo + K // 2], [rc], sem.s_in, off)
-        if root:
+        i, h = hs.index(core), (len(hs) + 1) // 2
+        b = 2 if i < h else 3
+        i, n = (i, h) if i < h else (i - h, len(hs) - h)
+        lo, hi = K * b + K // 2 * i // n * 2, K * b + K // 2 * (i + 1) // n * 2
+        make_pick(b)
+        send(u8(T.scode, lo, hi), [rc], sem.s_in, off)
+        send(T.splane[:, lo:hi], [rc], sem.s_in, off)
+        if core == hs[0]:
+            g.wait_ge(sem.hop_s, n_on)
+            send(pick_codes, [T.cores[peer]], sem.s_in, off)
+        for hop, t, dst, rsem in ([(ahop, at, adst, sem.a_in)] if root else []) + [(vhop, vt, vdst, sem["arr%d" % s])]:
             for w in (0, 1):
-                g.wait_ge(ahop[w], n_on)
-                send(at[w], adst, sem.a_in, off)
-        for w in (0, 1):
-            g.wait_ge(vhop[w], n_on)
-            send(vt[w], vdst, sem["arr%d" % s], off)
+                if dst[w]:
+                    g.wait_ge(hop[w], n_on)
+                    send(t[w], dst[w], rsem, off)
         g.wait_ge(sem.sent, sent[0])
         return
 
-    def spread(t, dests, hop, rsem):
+    def to_helpers(t, hop):
         for w in (0, 1):
-            send(t[w], hs, hop[w], on)
+            send(t[w], hop_to[w], hop[w], on)
+
+    def to_ranks(t, dests, rsem):
         for w in (0, 1):
-            send(t[w], dests, rsem, off)
+            send(t[w], dests[w], rsem, off)
 
     if root:
         g.sync.dma_start(T.a16[:], T.a[:]).then_inc(sem.ld_a, 16)
-        g.sync.wait_ge(sem.ld_a, 16)
+    g.sync.dma_start(T.b16[:], T.bb[:]).then_inc(sem.ld_b, 16)
     g.sync.dma_start(u8(T.wcode, 0, K), T.wc[:]).then_inc(sem.ld_w, 16)
     g.sync.dma_start(T.wplane[:], T.ws[:]).then_inc(sem.ld_w, 16)
-    g.sync.dma_start(T.b16[:], T.bb[:]).then_inc(sem.ld_b, 16)
     g.sync.dma_start(T.x16[:], T.x[:]).then_inc(sem.ld_x, 16)
 
+    make_pick(pick)
+    send(pick_codes, hs[:1], sem.hop_s, on)
     if root:
         g.vector.wait_ge(sem.ld_a, 16)
         g.vector.quantize_mx(T.acode[:], T.aplane[:], T.a16[:]).then_inc(sem.qa, 1)
         g.wait_ge(sem.qa, 1)
-        spread(at, adst, ahop, sem.a_in)
-    tiles, peer, give, get = own_picks(T, s)
-    make_picks(tiles)
-    for b in give:
-        send(u8(T.scode, K * b, K * b + K), [T.cores[peer]], sem.s_in, off)
-        send(T.splane[:, K * b:K * b + K], [T.cores[peer]], sem.s_in, off)
+        to_helpers(at, ahop)
+    send(T.splane[:, K * pick:K * pick + K], [T.cores[peer]], sem.s_in, off)
+    if root:
+        to_ranks(at, adst, sem.a_in)
 
     g.vector.wait_ge(sem.ld_b, 16)
     for b in range(4):
@@ -171,9 +183,8 @@ def rank_program(g, core, T, topo):
 
     te = g.tensor
     te.wait_ge(sem.ld_w, 32)
-    if tiles:
-        te.wait_ge(sem.qs, len(tiles))
-    te.wait_ge(sem.s_in, 2 * n_off * (len(get) + len(hs)))
+    te.wait_ge(sem.qs, 1)
+    te.wait_ge(sem.s_in, 2 * n_off * (1 + len(hs)))
     for b in range(4):
         te.matmul_mx(bank(b), T.scode[:, K * b:K * b + K], T.splane[:, K * b:K * b + K], T.wcode[:], T.wplane[:],
                      True, True).then_inc(sem.dmm, 1)
@@ -187,9 +198,13 @@ def rank_program(g, core, T, topo):
                      True, True).then_inc(sem["mm%d" % b], 1)
 
     for b in range(4):
-        g.scalar.wait_ge(sem["mm%d" % b], 1)
-        g.scalar.activation(T.scaled[:, K * b:K * b + K], bank(4 + b), ActivationFunctionType.Copy,
-                            scale=0.047).then_inc(sem["mu%d" % b], 1)
+        q = g.vector if b == 1 else g.scalar
+        q.wait_ge(sem["mm%d" % b], 1)
+        dst = T.scaled[:, K * b:K * b + K]
+        if b == 1:
+            q.tensor_scalar(dst, bank(4 + b), 0.047, None, AluOpType.mult).then_inc(sem["mu%d" % b], 1)
+        else:
+            q.activation(dst, bank(4 + b), ActivationFunctionType.Copy, scale=0.047).then_inc(sem["mu%d" % b], 1)
     g.vector.wait_ge(sem.dmm, 4)
     for b in range(4):
         g.vector.wait_ge(sem["mu%d" % b], 1)
@@ -198,9 +213,12 @@ def rank_program(g, core, T, topo):
     g.vector.wait_ge(sem.added, 4)
     g.vector.quantize_mx(T.vcode[:, K * s:K * s + K], T.vplane[:, K * s:K * s + K], T.v16[:]).then_inc(sem.qv, 1)
     g.wait_ge(sem.qv, 1)
-    spread(vt, vdst, vhop, sem["arr%d" % s])
+    to_helpers(vt, vhop)
+    to_ranks(vt, vdst, sem["arr%d" % s])
 
-    order = [s] + [j for _, j in sorted((due(T, topo, j, s), j) for j in range(N) if j != s)]
+    adue = eta(aroute)
+    due = {j: adue.get(j, 0.0) + eta(plan(T, topo, j))[s] for j in range(N) if j != s}
+    order = [s] + sorted(due, key=lambda j: (due[j], j))
     te.wait_ge(sem.qx, 1)
     for t, j in enumerate(order):
         if j == s:
@@ -222,7 +240,7 @@ def rank_program(g, core, T, topo):
     left, stores = list(order), 0
     while left:
         grp = [left.pop(0)]
-        near = [q for q in left[:3] if abs(q - grp[0]) == 1]
+        near = [q for q in left[:2] if abs(q - grp[0]) == 1]
         if near and len(left) > 1:
             grp.append(near[0])
             left.remove(near[0])

from concourse.bass import DstId, RemoteDMATransfer
from concourse.mybir import dt, AluOpType, ActivationFunctionType

N = 16
K = 128
FP8 = "float8_e4m3fn_x4"
WORLD = 256
ON, OFF, HOP = (0.12, 0.22), (0.25, 0.5), 0.9

SCRATCH = {
    "a16": ("sbuf", [128, 4 * K], "bfloat16"),
    "b16": ("sbuf", [128, 16 * K], "bfloat16"),
    "x16": ("sbuf", [128, 4 * K], "bfloat16"),
    "sel": ("sbuf", [128, 4 * K], "bfloat16"),
    "v16": ("sbuf", [128, 4 * K], "bfloat16"),
    "acode": ("sbuf", [128, K], FP8), "aplane": ("sbuf", [128, K], "uint8"),
    "bcode": ("sbuf", [128, 4 * K], FP8), "bplane": ("sbuf", [128, 4 * K], "uint8"),
    "xcode": ("sbuf", [128, K], FP8), "xplane": ("sbuf", [128, K], "uint8"),
    "wcode": ("sbuf", [128, K], FP8), "wplane": ("sbuf", [128, K], "uint8"),
    "scode": ("sbuf", [128, 4 * K], FP8), "splane": ("sbuf", [128, 4 * K], "uint8"),
    "vcode": ("sbuf", [128, N * K], FP8), "vplane": ("sbuf", [128, N * K], "uint8"),
    "scaled": ("sbuf", [128, 4 * K], "float32"),
    "yo": ("sbuf", [128, N * K], "float32"),
    "ps": ("psum", [128, 512 * 8], "float32"),
}
SEMAPHORES = (["ld_a", "ld_w", "ld_b", "ld_x", "ones", "diag", "qs", "qa", "qb", "qx", "qv",
               "s_in", "hop_s", "a_in", "hop_ac", "hop_ap", "hop_vc", "hop_vp", "sent", "dmm", "added", "st"]
              + ["arr%d" % j for j in range(N)] + ["mm%d" % b for b in range(4)] + ["mu%d" % b for b in range(4)]
              + ["ym%d" % t for t in range(N)] + ["yc%d" % t for t in range(N)])


def chip_of(topo, c):
    return (topo.host(c), topo.chip(c))


def plan(T, topo, s):
    rc = T.cores[s]
    others = [(s + k) % N for k in range(1, N)]
    here = [c for c in range(WORLD) if c != rc and chip_of(topo, c) == chip_of(topo, rc)]
    free = [c for c in here if all(topo.may_write(c, T.cores[d]) for d in others)]
    def by_die(cores):
        return [[c for c in cores if (topo.die(c) == topo.die(rc)) == near] for near in (False, True)]
    (f0, f1), (n0, n1) = by_die(free)
    bf, bn = by_die([c for c in here if c not in free])
    same = [d for d in others if topo.may_write(rc, T.cores[d])]
    cross = [d for d in others if d not in same]
    if len(cross) < len(same):
        fs, ns, fc, nc = same[:4], same[4:], cross[:3], cross[3:]
    else:
        fs, ns, fc, nc = same[:2], same[2:], cross[:5], cross[5:]
    codes = {f0: fc[:3], n0: nc[:3], bf[0]: fs[:2], bn[0]: ns[:3], bf[1]: fs[2:], f1: fc[3:], n1: nc[3:], rc: ns[3:]}
    if codes[f1]:
        planes = {f1: nc, n1: fc, rc: same}
    else:
        planes = {f1: nc + ns, n1: fc + fs}
    route = [(c, planes.get(c, []), codes[c]) for c in [rc, f0, n0, bf[0], bn[0], bf[1], f1, n1]]
    return [r for r in route if r[1] or r[2]]


def eta(route):
    t, due, start = 0.0, {}, {}
    for w in (0, 1):
        for c, *lists in route[1:]:
            if lists[w]:
                t += ON[w]
                start[c, w] = t + HOP
    for c, *lists in route:
        u = t
        for w in (0, 1):
            u = max(u, start.get((c, w), 0.0))
            for d in lists[w]:
                u += OFF[w]
                due[d] = max(due.get(d, 0.0), u)
    return due


def own_pick(r):
    p = (r + N // 2) % N
    return (0 if r < p else 1), p


def u8(buf, a, b):
    return buf[:, a:b].bitcast(dt.uint8)


def rank_program(g, core, T, topo):
    mine = [s for s in range(N) if chip_of(topo, T.cores[s]) == chip_of(topo, core)]
    if not mine:
        return
    s = mine[0]
    vroute, aroute = plan(T, topo, s), plan(T, topo, T.root)
    vdst = [[T.cores[d] for d in ds] for c, *lists in vroute if c == core for ds in lists]
    adst = [[T.cores[d] for d in ds] for c, *lists in aroute if c == core for ds in lists]
    if not vdst:
        return
    rc, root, sem = T.cores[s], s == T.root, T.sem
    hs = [c for c, _, _ in vroute[1:]]
    hop_to = [[c for c, *lists in vroute[1:] if lists[w]] for w in (0, 1)]
    on, off = topo.mask(rc, hs[0]), topo.mask(core, (vdst[0] + vdst[1])[0])
    n_on, n_off = bin(on).count("1"), bin(off).count("1")
    sent = [0]

    def send(view, dests, rsem, m):
        if not dests:
            return
        ids = []
        for d in dests:
            rid, pid = topo.addr(d, core)
            ids.append(DstId(rid=rid, pnc=pid))
        g.remote_dma_fused([RemoteDMATransfer(dst_ids=ids, dma_engine_mask=m, remote_sem=rsem, srcs=[view],
                                              dsts=[view] * len(dests))], local_sem=sem.sent)
        sent[0] += bin(m).count("1")

    def make_pick(b):
        g.vector.memset(T.sel[:], 0.0).then_inc(sem.ones, 1)
        g.wait_ge(sem.ones, 1)
        v = T.sel[:, b:4 * K:4]
        g.affine_select(v, v, [[1, K]], AluOpType.not_equal, 1.0, 0, -1).then_inc(sem.diag, 1)
        g.vector.wait_ge(sem.diag, 1)
        g.vector.quantize_mx(T.scode[:, K * b:K * b + K], T.splane[:, K * b:K * b + K], T.sel[:]).then_inc(sem.qs, 1)
        g.wait_ge(sem.qs, 1)

    vt = (T.vplane[:, K * s:K * s + K], u8(T.vcode, K * s, K * s + K))
    at = (T.aplane[:, 0:K], u8(T.acode, 0, K))
    vhop, ahop = (sem.hop_vp, sem.hop_vc), (sem.hop_ap, sem.hop_ac)
    pick, peer = own_pick(s)
    pick_codes = u8(T.scode, K * pick, K * pick + K)

    if core != rc:
        i, h = hs.index(core), (len(hs) + 1) // 2
        b = 2 if i < h else 3
        i, n = (i, h) if i < h else (i - h, len(hs) - h)
        lo, hi = K * b + K // 2 * i // n * 2, K * b + K // 2 * (i + 1) // n * 2
        make_pick(b)
        send(u8(T.scode, lo, hi), [rc], sem.s_in, off)
        send(T.splane[:, lo:hi], [rc], sem.s_in, off)
        if core == hs[0]:
            g.wait_ge(sem.hop_s, n_on)
            send(pick_codes, [T.cores[peer]], sem.s_in, off)
        for hop, t, dst, rsem in ([(ahop, at, adst, sem.a_in)] if root else []) + [(vhop, vt, vdst, sem["arr%d" % s])]:
            for w in (0, 1):
                if dst[w]:
                    g.wait_ge(hop[w], n_on)
                    send(t[w], dst[w], rsem, off)
        g.wait_ge(sem.sent, sent[0])
        return

    def to_helpers(t, hop):
        for w in (0, 1):
            send(t[w], hop_to[w], hop[w], on)

    def to_ranks(t, dests, rsem):
        for w in (0, 1):
            send(t[w], dests[w], rsem, off)

    if root:
        g.sync.dma_start(T.a16[:], T.a[:]).then_inc(sem.ld_a, 16)
    g.sync.dma_start(T.b16[:], T.bb[:]).then_inc(sem.ld_b, 16)
    g.sync.dma_start(u8(T.wcode, 0, K), T.wc[:]).then_inc(sem.ld_w, 16)
    g.sync.dma_start(T.wplane[:], T.ws[:]).then_inc(sem.ld_w, 16)
    g.sync.dma_start(T.x16[:], T.x[:]).then_inc(sem.ld_x, 16)

    make_pick(pick)
    send(pick_codes, hs[:1], sem.hop_s, on)
    if root:
        g.vector.wait_ge(sem.ld_a, 16)
        g.vector.quantize_mx(T.acode[:], T.aplane[:], T.a16[:]).then_inc(sem.qa, 1)
        g.wait_ge(sem.qa, 1)
        to_helpers(at, ahop)
    send(T.splane[:, K * pick:K * pick + K], [T.cores[peer]], sem.s_in, off)
    if root:
        to_ranks(at, adst, sem.a_in)

    g.vector.wait_ge(sem.ld_b, 16)
    for b in range(4):
        g.vector.quantize_mx(T.bcode[:, K * b:K * b + K], T.bplane[:, K * b:K * b + K],
                             T.b16[:, 4 * K * b:4 * K * (b + 1)]).then_inc(sem.qb, 1)
    g.vector.wait_ge(sem.ld_x, 16)
    g.vector.quantize_mx(T.xcode[:], T.xplane[:], T.x16[:]).then_inc(sem.qx, 1)

    def bank(i):
        return T.ps[:, 512 * i:512 * i + K]

    te = g.tensor
    te.wait_ge(sem.ld_w, 32)
    te.wait_ge(sem.qs, 1)
    te.wait_ge(sem.s_in, 2 * n_off * (1 + len(hs)))
    for b in range(4):
        te.matmul_mx(bank(b), T.scode[:, K * b:K * b + K], T.splane[:, K * b:K * b + K], T.wcode[:], T.wplane[:],
                     True, True).then_inc(sem.dmm, 1)
    te.wait_ge(sem.qb, 4)
    if root:
        te.wait_ge(sem.qa, 1)
    else:
        te.wait_ge(sem.a_in, 2 * n_off)
    for b in range(4):
        te.matmul_mx(bank(4 + b), T.bcode[:, K * b:K * b + K], T.bplane[:, K * b:K * b + K], T.acode[:], T.aplane[:],
                     True, True).then_inc(sem["mm%d" % b], 1)

    for b in range(4):
        q = g.vector if b == 1 else g.scalar
        q.wait_ge(sem["mm%d" % b], 1)
        dst = T.scaled[:, K * b:K * b + K]
        if b == 1:
            q.tensor_scalar(dst, bank(4 + b), 0.047, None, AluOpType.mult).then_inc(sem["mu%d" % b], 1)
        else:
            q.activation(dst, bank(4 + b), ActivationFunctionType.Copy, scale=0.047).then_inc(sem["mu%d" % b], 1)
    g.vector.wait_ge(sem.dmm, 4)
    for b in range(4):
        g.vector.wait_ge(sem["mu%d" % b], 1)
        g.vector.tensor_tensor(T.v16[:, b:4 * K:4], bank(b), T.scaled[:, K * b:K * b + K],
                               AluOpType.add).then_inc(sem.added, 1)
    g.vector.wait_ge(sem.added, 4)
    g.vector.quantize_mx(T.vcode[:, K * s:K * s + K], T.vplane[:, K * s:K * s + K], T.v16[:]).then_inc(sem.qv, 1)
    g.wait_ge(sem.qv, 1)
    to_helpers(vt, vhop)
    to_ranks(vt, vdst, sem["arr%d" % s])

    adue = eta(aroute)
    due = {j: adue.get(j, 0.0) + eta(plan(T, topo, j))[s] for j in range(N) if j != s}
    order = [s] + sorted(due, key=lambda j: (due[j], j))
    te.wait_ge(sem.qx, 1)
    for t, j in enumerate(order):
        if j == s:
            te.wait_ge(sem.qv, 1)
        else:
            te.wait_ge(sem["arr%d" % j], 2 * n_off)
        if t >= 8:
            te.wait_ge(sem["yc%d" % (t - 8)], 1)
        te.matmul_mx(bank(t % 8), T.vcode[:, K * j:K * j + K], T.vplane[:, K * j:K * j + K], T.xcode[:], T.xplane[:],
                     True, True).then_inc(sem["ym%d" % t], 1)
        dst = T.yo[:, K * j:K * j + K]
        if t % 2:
            g.scalar.wait_ge(sem["ym%d" % t], 1)
            g.scalar.activation(dst, bank(t % 8), ActivationFunctionType.Copy).then_inc(sem["yc%d" % t], 1)
        else:
            g.vector.wait_ge(sem["ym%d" % t], 1)
            g.vector.tensor_copy(dst, bank(t % 8)).then_inc(sem["yc%d" % t], 1)

    left, stores = list(order), 0
    while left:
        grp = [left.pop(0)]
        near = [q for q in left[:2] if abs(q - grp[0]) == 1]
        if near and len(left) > 1:
            grp.append(near[0])
            left.remove(near[0])
        for q in grp:
            g.sync.wait_ge(sem["yc%d" % order.index(q)], 1)
        lo, hi = K * min(grp), K * (max(grp) + 1)
        g.sync.dma_start(T.y[:, lo:hi], T.yo[:, lo:hi]).then_inc(sem.st, 16)
        stores += 1
    g.sync.wait_ge(sem.st, 16 * stores)
    g.wait_ge(sem.sent, sent[0])
